import numpy as np
import ml_dtypes


def mxq(x, axis, fmt="e4m3"):
    dtype, down = {"e4m3": (ml_dtypes.float8_e4m3fn, 7), "e5m2": (ml_dtypes.float8_e5m2, 14)}[fmt]
    v = np.moveaxis(np.asarray(x, np.float32).astype(ml_dtypes.bfloat16).astype(np.float64), axis, -1)
    blocks = v.reshape(v.shape[:-1] + (-1, 32))
    amax = np.abs(blocks).max(-1, keepdims=True)
    byte = np.maximum(np.where(amax > 0, np.frexp(amax)[1] - 1 + 127, 0) - down, 1)
    scale = np.exp2(byte - 127.0)
    codes = (blocks / scale).astype(np.float32).astype(dtype).astype(np.float64)
    return np.moveaxis((codes * scale).reshape(v.shape), -1, axis)


WIDE = False


def mx_kscale(k):
    if not WIDE:
        return np.ones(k)
    levels = np.array([10, -10, 5, -5, 0])
    if k % 512:
        return np.exp2(np.random.permutation(np.resize(levels, k // 32))).repeat(32)
    a = np.empty((k // 512, 16))
    for p in range(k // 512):
        a[p, :8] = np.random.permutation(np.resize(levels, 8))
        for g in range(8):
            far = levels[np.abs(levels - a[p, g]) >= 10]
            a[p, g + 8] = far[np.random.randint(len(far))]
    return np.exp2(a.ravel()).repeat(32)


def f64(x):
    return np.asarray(x).astype(np.float64)


def striped8(idx):
    return np.concatenate([v.reshape(-1, 16).T for v in idx]).astype(np.uint16)


def unstriped8(offs):
    return np.stack([offs[16 * g:16 * g + 16].T.reshape(-1) for g in range(8)]).astype(np.int64)


K, M, T, S = 1536, 1024, 1024, 512


def setup_inputs():
    n = np.random.standard_normal
    s = mx_kscale(K)[:, None]
    return {
        "xT": (n((K, T)) * s).astype(np.float32),
        "w": (n((K, M)) / np.sqrt(K) / s).astype(np.float32),
        "wgt": np.repeat(np.random.uniform(0.5, 2.0, (8, S)), 16, axis=0).astype(np.float32),
        "r": (n((1024, 512))).astype(np.float32),
        "offs": striped8(np.stack([np.random.permutation(T)[:S] for _ in range(8)])),
    }


def reference(xT, w, wgt, r, offs):
    idx = unstriped8(offs)
    group = np.arange(K) % 512 // 64
    xg = f64(wgt)[np.arange(K) // 4 % 128] * f64(xT)[np.arange(K)[:, None], idx[group]]
    xT_ = mxq(xg, 0, "e4m3")
    w_ = mxq(f64(w), 0, "e4m3")
    y = w_.T @ xT_
    return f64(r) + y

@@ -1,0 +1,210 @@
+from contextlib import ExitStack
+
+import concourse.mybir as mybir
+
+K, M, T, S = 1536, 1024, 1024, 512
+FLOPS = 2 * K * M * S
+
+F32 = mybir.dt.float32
+BF16 = mybir.dt.bfloat16
+U32 = mybir.dt.uint32
+U16 = mybir.dt.uint16
+U8 = mybir.dt.uint8
+FP8X4 = mybir.dt.float8_e4m3fn_x4
+ADD = mybir.AluOpType.add
+MULT = mybir.AluOpType.mult
+
+P = 128
+PASSES = K // 512
+HALF_S = S // 2
+HALF_M = M // 2
+
+
+def tile_list_heads_res_kernel(tc, xT, w, wgt, r, offs, out):
+    nc = tc.nc
+    with ExitStack() as ctx:
+        keep = ctx.enter_context(tc.tile_pool(name="keep", bufs=1))
+        psum = ctx.enter_context(tc.psum_pool(name="psum", bufs=1))
+
+        offsets = keep.tile([P, S // 16], U16, name="offsets")
+        weights = keep.tile([P, S], F32, name="weights")
+        planes = [
+            [keep.tile([P, T], F32, name=f"x_{a}_{i}") for i in range(4)]
+            for a in range(PASSES)
+        ]
+        w_raw = [
+            [keep.tile([P, 4, HALF_M], F32, name=f"w_raw_{a}_{h}") for h in range(2)]
+            for a in range(PASSES)
+        ]
+        r_sb = [keep.tile([P, 4, S], F32, name=f"r_{h}") for h in range(2)]
+        out_sb = [keep.tile([P, S], F32, name=f"out_{m}") for m in range(8)]
+        picked = [
+            [keep.tile([P, 4, HALF_S], F32, name=f"picked_{a}_{s}") for s in range(2)]
+            for a in range(PASSES)
+        ]
+        x_bf = [
+            [keep.tile([P, HALF_S, 4], BF16, name=f"x_bf_{a}_{s}", align_bytes=64) for s in range(2)]
+            for a in range(PASSES)
+        ]
+        x_codes = [keep.tile([P, S], U32, name=f"x_codes_{a}", align_bytes=64) for a in range(PASSES)]
+        x_scales = [keep.tile([P, S], U8, name=f"x_scales_{a}", align_bytes=64) for a in range(PASSES)]
+        w_bf = [
+            [keep.tile([P, HALF_M, 4], BF16, name=f"w_bf_{a}_{h}", align_bytes=64) for h in range(2)]
+            for a in range(PASSES)
+        ]
+        w_codes = [keep.tile([P, M], U32, name=f"w_codes_{a}", align_bytes=64) for a in range(PASSES)]
+        w_scales = [keep.tile([P, M], U8, name=f"w_scales_{a}", align_bytes=64) for a in range(PASSES)]
+        acc = [psum.tile([P, S], F32, name=f"acc_{m}") for m in range(8)]
+
+        x_rows = xT.rearrange("(a p i) t -> a i p t", p=P, i=4)
+        w_rows = w.rearrange("(a p i) n -> a p i n", p=P, i=4)
+
+        def load_x(a, i):
+            nc.sync.dma_start(out=planes[a][i][:], in_=x_rows[a, i])
+
+        def load_w(a, h):
+            nc.sync.dma_start(out=w_raw[a][h][:], in_=w_rows[a, :, :, h * HALF_M : (h + 1) * HALF_M])
+
+        def load_r(m):
+            nc.sync.dma_start(out=r_sb[m // 4][:, m % 4, :], in_=r[m * P : (m + 1) * P, :])
+
+        def gather(a, i):
+            for s in range(2):
+                columns = offsets[:, s * 16 : (s + 1) * 16]
+                nc.vector.tensor_tensor(
+                    picked[a][s][:, i, :],
+                    planes[a][i][:].indirect(columns),
+                    weights[:, s * HALF_S : (s + 1) * HALF_S],
+                    MULT,
+                )
+
+        def interleave_x(copy, a, s):
+            copy(
+                out=x_bf[a][s][:].rearrange("p (c q) i -> p c i q", q=4),
+                in_=picked[a][s][:].rearrange("p i (c q) -> p c i q", q=4),
+            )
+
+        def quantise_x(a, s):
+            columns = slice(s * HALF_S, (s + 1) * HALF_S)
+            nc.vector.quantize_mx(
+                out=x_codes[a][:, columns].bitcast(FP8X4),
+                scales=x_scales[a][:, columns],
+                in_=x_bf[a][s][:].rearrange("p c i -> p (c i)"),
+            )
+
+        def interleave_w(copy, a, h, c0, c1):
+            copy(
+                out=w_bf[a][h][:, c0:c1, :].rearrange("p (c q) i -> p c i q", q=4),
+                in_=w_raw[a][h][:, :, c0:c1].rearrange("p i (c q) -> p c i q", q=4),
+            )
+
+        def quantise_w(a, h, c0, c1):
+            columns = slice(h * HALF_M + c0, h * HALF_M + c1)
+            nc.vector.quantize_mx(
+                out=w_codes[a][:, columns].bitcast(FP8X4),
+                scales=w_scales[a][:, columns],
+                in_=w_bf[a][h][:, c0:c1, :].rearrange("p c i -> p (c i)"),
+            )
+
+        def multiply(a, m):
+            columns = slice(m * P, (m + 1) * P)
+            nc.tensor.matmul_mx(
+                out=acc[m][:],
+                lhsT=w_codes[a][:, columns].bitcast(FP8X4),
+                lhsT_scale=w_scales[a][:, columns],
+                rhs=x_codes[a][:].bitcast(FP8X4),
+                rhs_scale=x_scales[a][:],
+                start=(a == 0),
+                stop=(a == PASSES - 1),
+            )
+
+        def finish(m):
+            nc.vector.tensor_tensor(out_sb[m][:], acc[m][:], r_sb[m // 4][:, m % 4, :], ADD)
+            nc.sync.dma_start(out=out[m * P : (m + 1) * P, :], in_=out_sb[m][:])
+
+        vec = nc.vector.tensor_copy
+        act = nc.scalar.copy
+
+        nc.sync.dma_start(offsets[:], offs)
+        nc.sync.dma_start(out=weights[:], in_=wgt)
+        load_x(0, 0)
+        load_x(0, 1)
+        load_w(0, 0)
+        load_x(0, 2)
+        load_x(0, 3)
+        load_w(0, 1)
+        for i in range(4):
+            load_x(1, i)
+        load_w(1, 0)
+        load_x(2, 0)
+        load_x(2, 1)
+        load_w(1, 1)
+        load_x(2, 2)
+        load_x(2, 3)
+        load_w(2, 0)
+        for m in range(4):
+            load_r(m)
+        load_w(2, 1)
+        for m in range(4, 8):
+            load_r(m)
+
+        gather(0, 0)
+        gather(0, 1)
+        interleave_w(act, 0, 0, 0, 256)
+        interleave_w(act, 0, 0, 256, 512)
+        gather(0, 2)
+        gather(0, 3)
+        quantise_w(0, 0, 0, 512)
+        interleave_x(act, 0, 0)
+        interleave_x(act, 0, 1)
+        gather(1, 0)
+        quantise_x(0, 0)
+        quantise_x(0, 1)
+        interleave_w(act, 0, 1, 0, 256)
+        interleave_w(act, 0, 1, 256, 512)
+        gather(1, 1)
+        gather(1, 2)
+        quantise_w(0, 1, 0, 512)
+        for m in range(8):
+            multiply(0, m)
+        gather(1, 3)
+        interleave_x(act, 1, 0)
+        interleave_x(act, 1, 1)
+        interleave_w(act, 1, 0, 0, 256)
+        interleave_w(act, 1, 0, 256, 512)
+        gather(2, 0)
+        quantise_x(1, 0)
+        quantise_x(1, 1)
+        gather(2, 1)
+        quantise_w(1, 0, 0, 512)
+        interleave_w(act, 1, 1, 0, 256)
+        interleave_w(act, 1, 1, 256, 512)
+        gather(2, 2)
+        gather(2, 3)
+        quantise_w(1, 1, 0, 512)
+        for m in range(8):
+            multiply(1, m)
+        interleave_x(act, 2, 0)
+        interleave_x(vec, 2, 1)
+        interleave_w(vec, 2, 0, 0, 256)
+        interleave_w(act, 2, 0, 256, 512)
+        quantise_x(2, 1)
+        quantise_x(2, 0)
+        quantise_w(2, 0, 0, 256)
+        quantise_w(2, 0, 256, 512)
+        for m in range(4):
+            multiply(2, m)
+        finish(0)
+        finish(1)
+        interleave_w(vec, 2, 1, 0, 256)
+        interleave_w(act, 2, 1, 256, 384)
+        finish(2)
+        quantise_w(2, 1, 0, 256)
+        interleave_w(act, 2, 1, 384, 512)
+        finish(3)
+        quantise_w(2, 1, 256, 384)
+        quantise_w(2, 1, 384, 512)
+        for m in range(4, 8):
+            multiply(2, m)
+        for m in range(4, 8):
+            finish(m)

@@ -17,7 +17,6 @@ MULT = mybir.AluOpType.mult
 P = 128
 PASSES = K // 512
 HALF_S = S // 2
-HALF_M = M // 2
 
 
 def tile_list_heads_res_kernel(tc, xT, w, wgt, r, offs, out):
@@ -32,11 +31,9 @@ def tile_list_heads_res_kernel(tc, xT, w, wgt, r, offs, out):
             [keep.tile([P, T], F32, name=f"x_{a}_{i}") for i in range(4)]
             for a in range(PASSES)
         ]
-        w_raw = [
-            [keep.tile([P, 4, HALF_M], F32, name=f"w_raw_{a}_{h}") for h in range(2)]
-            for a in range(PASSES)
-        ]
-        r_sb = [keep.tile([P, 4, S], F32, name=f"r_{h}") for h in range(2)]
+        w_raw = [keep.tile([P, 4, M], F32, name=f"w_raw_{a}") for a in range(PASSES - 1)]
+        w_last = [keep.tile([P, 4, M // 2], F32, name=f"w_last_{h}") for h in range(2)]
+        r_sb = [keep.tile([P, 2, S], F32, name=f"r_{q}") for q in range(4)]
         out_sb = [keep.tile([P, S], F32, name=f"out_{m}") for m in range(8)]
         picked = [
             [keep.tile([P, 4, HALF_S], F32, name=f"picked_{a}_{s}") for s in range(2)]
@@ -48,25 +45,23 @@ def tile_list_heads_res_kernel(tc, xT, w, wgt, r, offs, out):
         ]
         x_codes = [keep.tile([P, S], U32, name=f"x_codes_{a}", align_bytes=64) for a in range(PASSES)]
         x_scales = [keep.tile([P, S], U8, name=f"x_scales_{a}", align_bytes=64) for a in range(PASSES)]
-        w_bf = [
-            [keep.tile([P, HALF_M, 4], BF16, name=f"w_bf_{a}_{h}", align_bytes=64) for h in range(2)]
-            for a in range(PASSES)
-        ]
+        w_bf = [keep.tile([P, M, 4], BF16, name=f"w_bf_{a}", align_bytes=64) for a in range(PASSES)]
         w_codes = [keep.tile([P, M], U32, name=f"w_codes_{a}", align_bytes=64) for a in range(PASSES)]
         w_scales = [keep.tile([P, M], U8, name=f"w_scales_{a}", align_bytes=64) for a in range(PASSES)]
         acc = [psum.tile([P, S], F32, name=f"acc_{m}") for m in range(8)]
 
         x_rows = xT.rearrange("(a p i) t -> a i p t", p=P, i=4)
         w_rows = w.rearrange("(a p i) n -> a p i n", p=P, i=4)
+        r_rows = r.rearrange("(q e p) j -> q p e j", p=P, e=2)
 
         def load_x(a, i):
             nc.sync.dma_start(out=planes[a][i][:], in_=x_rows[a, i])
 
-        def load_w(a, h):
-            nc.sync.dma_start(out=w_raw[a][h][:], in_=w_rows[a, :, :, h * HALF_M : (h + 1) * HALF_M])
+        def load_w(a):
+            nc.sync.dma_start(out=w_raw[a][:], in_=w_rows[a])
 
-        def load_r(m):
-            nc.sync.dma_start(out=r_sb[m // 4][:, m % 4, :], in_=r[m * P : (m + 1) * P, :])
+        def load_r(q):
+            nc.sync.dma_start(out=r_sb[q][:], in_=r_rows[q])
 
         def gather(a, i):
             for s in range(2):
@@ -92,18 +87,22 @@ def tile_list_heads_res_kernel(tc, xT, w, wgt, r, offs, out):
                 in_=x_bf[a][s][:].rearrange("p c i -> p (c i)"),
             )
 
-        def interleave_w(copy, a, h, c0, c1):
+        def interleave_w(copy, a, c):
+            columns = slice(c * 256, (c + 1) * 256)
+            if a < PASSES - 1:
+                raw = w_raw[a][:, :, columns]
+            else:
+                raw = w_last[c // 2][:, :, c % 2 * 256 : (c % 2 + 1) * 256]
             copy(
-                out=w_bf[a][h][:, c0:c1, :].rearrange("p (c q) i -> p c i q", q=4),
-                in_=w_raw[a][h][:, :, c0:c1].rearrange("p i (c q) -> p c i q", q=4),
+                out=w_bf[a][:, columns, :].rearrange("p (c q) i -> p c i q", q=4),
+                in_=raw.rearrange("p i (c q) -> p c i q", q=4),
             )
 
-        def quantise_w(a, h, c0, c1):
-            columns = slice(h * HALF_M + c0, h * HALF_M + c1)
+        def quantise_w(a, c0, c1):
             nc.vector.quantize_mx(
-                out=w_codes[a][:, columns].bitcast(FP8X4),
-                scales=w_scales[a][:, columns],
-                in_=w_bf[a][h][:, c0:c1, :].rearrange("p c i -> p (c i)"),
+                out=w_codes[a][:, c0:c1].bitcast(FP8X4),
+                scales=w_scales[a][:, c0:c1],
+                in_=w_bf[a][:, c0:c1, :].rearrange("p c i -> p (c i)"),
             )
 
         def multiply(a, m):
@@ -119,7 +118,7 @@ def tile_list_heads_res_kernel(tc, xT, w, wgt, r, offs, out):
             )
 
         def finish(m):
-            nc.vector.tensor_tensor(out_sb[m][:], acc[m][:], r_sb[m // 4][:, m % 4, :], ADD)
+            nc.vector.tensor_tensor(out_sb[m][:], acc[m][:], r_sb[m // 2][:, m % 2, :], ADD)
             nc.sync.dma_start(out=out[m * P : (m + 1) * P, :], in_=out_sb[m][:])
 
         vec = nc.vector.tensor_copy
@@ -127,84 +126,77 @@ def tile_list_heads_res_kernel(tc, xT, w, wgt, r, offs, out):
 
         nc.sync.dma_start(offsets[:], offs)
         nc.sync.dma_start(out=weights[:], in_=wgt)
-        load_x(0, 0)
-        load_x(0, 1)
-        load_w(0, 0)
-        load_x(0, 2)
-        load_x(0, 3)
-        load_w(0, 1)
+        for i in range(4):
+            load_x(0, i)
         for i in range(4):
             load_x(1, i)
-        load_w(1, 0)
         load_x(2, 0)
         load_x(2, 1)
-        load_w(1, 1)
+        load_w(0)
         load_x(2, 2)
         load_x(2, 3)
-        load_w(2, 0)
-        for m in range(4):
-            load_r(m)
-        load_w(2, 1)
-        for m in range(4, 8):
-            load_r(m)
+        load_w(1)
+        for h in range(2):
+            nc.sync.dma_start(out=w_last[h][:], in_=w_rows[2, :, :, h * 512 : (h + 1) * 512])
+        for q in range(4):
+            load_r(q)
 
-        gather(0, 0)
-        gather(0, 1)
-        interleave_w(act, 0, 0, 0, 256)
-        interleave_w(act, 0, 0, 256, 512)
-        gather(0, 2)
-        gather(0, 3)
-        quantise_w(0, 0, 0, 512)
+        for i in range(4):
+            gather(0, i)
         interleave_x(act, 0, 0)
         interleave_x(act, 0, 1)
         gather(1, 0)
         quantise_x(0, 0)
         quantise_x(0, 1)
-        interleave_w(act, 0, 1, 0, 256)
-        interleave_w(act, 0, 1, 256, 512)
         gather(1, 1)
         gather(1, 2)
-        quantise_w(0, 1, 0, 512)
-        for m in range(8):
-            multiply(0, m)
         gather(1, 3)
         interleave_x(act, 1, 0)
         interleave_x(act, 1, 1)
-        interleave_w(act, 1, 0, 0, 256)
-        interleave_w(act, 1, 0, 256, 512)
         gather(2, 0)
         quantise_x(1, 0)
         quantise_x(1, 1)
         gather(2, 1)
-        quantise_w(1, 0, 0, 512)
-        interleave_w(act, 1, 1, 0, 256)
-        interleave_w(act, 1, 1, 256, 512)
+        interleave_w(act, 0, 0)
+        interleave_w(act, 0, 1)
+        interleave_w(act, 0, 2)
+        interleave_w(vec, 0, 3)
         gather(2, 2)
-        gather(2, 3)
-        quantise_w(1, 1, 0, 512)
+        quantise_w(0, 0, 512)
+        quantise_w(0, 512, 1024)
         for m in range(8):
-            multiply(1, m)
+            multiply(0, m)
+        gather(2, 3)
         interleave_x(act, 2, 0)
         interleave_x(vec, 2, 1)
-        interleave_w(vec, 2, 0, 0, 256)
-        interleave_w(act, 2, 0, 256, 512)
-        quantise_x(2, 1)
+        interleave_w(vec, 1, 0)
         quantise_x(2, 0)
-        quantise_w(2, 0, 0, 256)
-        quantise_w(2, 0, 256, 512)
-        for m in range(4):
-            multiply(2, m)
+        quantise_x(2, 1)
+        for c in range(1, 4):
+            interleave_w(act, 1, c)
+        for c in range(4):
+            quantise_w(1, 256 * c, 256 * (c + 1))
+            multiply(1, 2 * c)
+            multiply(1, 2 * c + 1)
+        interleave_w(vec, 2, 0)
+        interleave_w(act, 2, 1)
+        quantise_w(2, 0, 256)
+        multiply(2, 0)
+        multiply(2, 1)
+        quantise_w(2, 256, 512)
+        multiply(2, 2)
+        multiply(2, 3)
+        interleave_w(vec, 2, 2)
+        interleave_w(act, 2, 3)
         finish(0)
         finish(1)
-        interleave_w(vec, 2, 1, 0, 256)
-        interleave_w(act, 2, 1, 256, 384)
+        quantise_w(2, 512, 768)
+        multiply(2, 4)
+        multiply(2, 5)
         finish(2)
-        quantise_w(2, 1, 0, 256)
-        interleave_w(act, 2, 1, 384, 512)
         finish(3)
-        quantise_w(2, 1, 256, 384)
-        quantise_w(2, 1, 384, 512)
-        for m in range(4, 8):
-            multiply(2, m)
+        quantise_w(2, 768, 1024)
+        multiply(2, 6)
+        multiply(2, 7)
         for m in range(4, 8):
             finish(m)

@@ -39,10 +39,7 @@ def tile_list_heads_res_kernel(tc, xT, w, wgt, r, offs, out):
             [keep.tile([P, 4, HALF_S], F32, name=f"picked_{a}_{s}") for s in range(2)]
             for a in range(PASSES)
         ]
-        x_bf = [
-            [keep.tile([P, HALF_S, 4], BF16, name=f"x_bf_{a}_{s}", align_bytes=64) for s in range(2)]
-            for a in range(PASSES)
-        ]
+        x_bf = [keep.tile([P, S, 4], BF16, name=f"x_bf_{a}", align_bytes=64) for a in range(PASSES)]
         x_codes = [keep.tile([P, S], U32, name=f"x_codes_{a}", align_bytes=64) for a in range(PASSES)]
         x_scales = [keep.tile([P, S], U8, name=f"x_scales_{a}", align_bytes=64) for a in range(PASSES)]
         w_bf = [keep.tile([P, M, 4], BF16, name=f"w_bf_{a}", align_bytes=64) for a in range(PASSES)]
@@ -74,17 +71,17 @@ def tile_list_heads_res_kernel(tc, xT, w, wgt, r, offs, out):
                 )
 
         def interleave_x(copy, a, s):
+            columns = slice(s * HALF_S, (s + 1) * HALF_S)
             copy(
-                out=x_bf[a][s][:].rearrange("p (c q) i -> p c i q", q=4),
+                out=x_bf[a][:, columns, :].rearrange("p (c q) i -> p c i q", q=4),
                 in_=picked[a][s][:].rearrange("p i (c q) -> p c i q", q=4),
             )
 
-        def quantise_x(a, s):
-            columns = slice(s * HALF_S, (s + 1) * HALF_S)
+        def quantise_x(a, c0, c1):
             nc.vector.quantize_mx(
-                out=x_codes[a][:, columns].bitcast(FP8X4),
-                scales=x_scales[a][:, columns],
-                in_=x_bf[a][s][:].rearrange("p c i -> p (c i)"),
+                out=x_codes[a][:, c0:c1].bitcast(FP8X4),
+                scales=x_scales[a][:, c0:c1],
+                in_=x_bf[a][:, c0:c1, :].rearrange("p c i -> p (c i)"),
             )
 
         def interleave_w(copy, a, c):
@@ -119,7 +116,8 @@ def tile_list_heads_res_kernel(tc, xT, w, wgt, r, offs, out):
 
         def finish(m):
             nc.vector.tensor_tensor(out_sb[m][:], acc[m][:], r_sb[m // 2][:, m % 2, :], ADD)
-            nc.sync.dma_start(out=out[m * P : (m + 1) * P, :], in_=out_sb[m][:])
+            queue = nc.scalar if m % 2 else nc.sync
+            queue.dma_start(out=out[m * P : (m + 1) * P, :], in_=out_sb[m][:])
 
         vec = nc.vector.tensor_copy
         act = nc.scalar.copy
@@ -146,32 +144,29 @@ def tile_list_heads_res_kernel(tc, xT, w, wgt, r, offs, out):
         interleave_x(act, 0, 0)
         interleave_x(act, 0, 1)
         gather(1, 0)
-        quantise_x(0, 0)
-        quantise_x(0, 1)
         gather(1, 1)
+        quantise_x(0, 0, 512)
         gather(1, 2)
         gather(1, 3)
         interleave_x(act, 1, 0)
         interleave_x(act, 1, 1)
         gather(2, 0)
-        quantise_x(1, 0)
-        quantise_x(1, 1)
         gather(2, 1)
+        quantise_x(1, 0, 512)
         interleave_w(act, 0, 0)
         interleave_w(act, 0, 1)
         interleave_w(act, 0, 2)
         interleave_w(vec, 0, 3)
         gather(2, 2)
-        quantise_w(0, 0, 512)
-        quantise_w(0, 512, 1024)
+        quantise_w(0, 0, 1024)
         for m in range(8):
             multiply(0, m)
         gather(2, 3)
         interleave_x(act, 2, 0)
         interleave_x(vec, 2, 1)
         interleave_w(vec, 1, 0)
-        quantise_x(2, 0)
-        quantise_x(2, 1)
+        quantise_x(2, 0, 256)
+        quantise_x(2, 256, 512)
         for c in range(1, 4):
             interleave_w(act, 1, c)
         for c in range(4):

from contextlib import ExitStack

import concourse.mybir as mybir

K, M, T, S = 1536, 1024, 1024, 512
FLOPS = 2 * K * M * S

F32 = mybir.dt.float32
BF16 = mybir.dt.bfloat16
U32 = mybir.dt.uint32
U16 = mybir.dt.uint16
U8 = mybir.dt.uint8
FP8X4 = mybir.dt.float8_e4m3fn_x4
ADD = mybir.AluOpType.add
MULT = mybir.AluOpType.mult

P = 128
PASSES = K // 512
HALF_S = S // 2


def tile_list_heads_res_kernel(tc, xT, w, wgt, r, offs, out):
    nc = tc.nc
    with ExitStack() as ctx:
        keep = ctx.enter_context(tc.tile_pool(name="keep", bufs=1))
        psum = ctx.enter_context(tc.psum_pool(name="psum", bufs=1))

        offsets = keep.tile([P, S // 16], U16, name="offsets")
        weights = keep.tile([P, S], F32, name="weights")
        planes = [
            [keep.tile([P, T], F32, name=f"x_{a}_{i}") for i in range(4)]
            for a in range(PASSES)
        ]
        w_raw = [keep.tile([P, 4, M], F32, name=f"w_raw_{a}") for a in range(PASSES - 1)]
        w_last = [keep.tile([P, 4, M // 2], F32, name=f"w_last_{h}") for h in range(2)]
        r_sb = [keep.tile([P, 2, S], F32, name=f"r_{q}") for q in range(4)]
        out_sb = [keep.tile([P, S], F32, name=f"out_{m}") for m in range(8)]
        picked = [
            [keep.tile([P, 4, HALF_S], F32, name=f"picked_{a}_{s}") for s in range(2)]
            for a in range(PASSES)
        ]
        x_bf = [keep.tile([P, S, 4], BF16, name=f"x_bf_{a}", align_bytes=64) for a in range(PASSES)]
        x_codes = [keep.tile([P, S], U32, name=f"x_codes_{a}", align_bytes=64) for a in range(PASSES)]
        x_scales = [keep.tile([P, S], U8, name=f"x_scales_{a}", align_bytes=64) for a in range(PASSES)]
        w_bf = [keep.tile([P, M, 4], BF16, name=f"w_bf_{a}", align_bytes=64) for a in range(PASSES)]
        w_codes = [keep.tile([P, M], U32, name=f"w_codes_{a}", align_bytes=64) for a in range(PASSES)]
        w_scales = [keep.tile([P, M], U8, name=f"w_scales_{a}", align_bytes=64) for a in range(PASSES)]
        acc = [psum.tile([P, S], F32, name=f"acc_{m}") for m in range(8)]

        x_rows = xT.rearrange("(a p i) t -> a i p t", p=P, i=4)
        w_rows = w.rearrange("(a p i) n -> a p i n", p=P, i=4)
        r_rows = r.rearrange("(q e p) j -> q p e j", p=P, e=2)

        def load_x(a, i):
            nc.sync.dma_start(out=planes[a][i][:], in_=x_rows[a, i])

        def load_w(a):
            nc.sync.dma_start(out=w_raw[a][:], in_=w_rows[a])

        def load_r(q):
            nc.sync.dma_start(out=r_sb[q][:], in_=r_rows[q])

        def gather(a, i):
            for s in range(2):
                columns = offsets[:, s * 16 : (s + 1) * 16]
                nc.vector.tensor_tensor(
                    picked[a][s][:, i, :],
                    planes[a][i][:].indirect(columns),
                    weights[:, s * HALF_S : (s + 1) * HALF_S],
                    MULT,
                )

        def interleave_x(copy, a, s):
            columns = slice(s * HALF_S, (s + 1) * HALF_S)
            copy(
                out=x_bf[a][:, columns, :].rearrange("p (c q) i -> p c i q", q=4),
                in_=picked[a][s][:].rearrange("p i (c q) -> p c i q", q=4),
            )

        def quantise_x(a, c0, c1):
            nc.vector.quantize_mx(
                out=x_codes[a][:, c0:c1].bitcast(FP8X4),
                scales=x_scales[a][:, c0:c1],
                in_=x_bf[a][:, c0:c1, :].rearrange("p c i -> p (c i)"),
            )

        def interleave_w(copy, a, c):
            columns = slice(c * 256, (c + 1) * 256)
            if a < PASSES - 1:
                raw = w_raw[a][:, :, columns]
            else:
                raw = w_last[c // 2][:, :, c % 2 * 256 : (c % 2 + 1) * 256]
            copy(
                out=w_bf[a][:, columns, :].rearrange("p (c q) i -> p c i q", q=4),
                in_=raw.rearrange("p i (c q) -> p c i q", q=4),
            )

        def quantise_w(a, c0, c1):
            nc.vector.quantize_mx(
                out=w_codes[a][:, c0:c1].bitcast(FP8X4),
                scales=w_scales[a][:, c0:c1],
                in_=w_bf[a][:, c0:c1, :].rearrange("p c i -> p (c i)"),
            )

        def multiply(a, m):
            columns = slice(m * P, (m + 1) * P)
            nc.tensor.matmul_mx(
                out=acc[m][:],
                lhsT=w_codes[a][:, columns].bitcast(FP8X4),
                lhsT_scale=w_scales[a][:, columns],
                rhs=x_codes[a][:].bitcast(FP8X4),
                rhs_scale=x_scales[a][:],
                start=(a == 0),
                stop=(a == PASSES - 1),
            )

        def finish(m):
            nc.vector.tensor_tensor(out_sb[m][:], acc[m][:], r_sb[m // 2][:, m % 2, :], ADD)
            queue = nc.scalar if m % 2 else nc.sync
            queue.dma_start(out=out[m * P : (m + 1) * P, :], in_=out_sb[m][:])

        vec = nc.vector.tensor_copy
        act = nc.scalar.copy

        nc.sync.dma_start(offsets[:], offs)
        nc.sync.dma_start(out=weights[:], in_=wgt)
        for i in range(4):
            load_x(0, i)
        for i in range(4):
            load_x(1, i)
        load_x(2, 0)
        load_x(2, 1)
        load_w(0)
        load_x(2, 2)
        load_x(2, 3)
        load_w(1)
        for h in range(2):
            nc.sync.dma_start(out=w_last[h][:], in_=w_rows[2, :, :, h * 512 : (h + 1) * 512])
        for q in range(4):
            load_r(q)

        for i in range(4):
            gather(0, i)
        interleave_x(act, 0, 0)
        interleave_x(act, 0, 1)
        gather(1, 0)
        gather(1, 1)
        quantise_x(0, 0, 512)
        gather(1, 2)
        gather(1, 3)
        interleave_x(act, 1, 0)
        interleave_x(act, 1, 1)
        gather(2, 0)
        gather(2, 1)
        quantise_x(1, 0, 512)
        interleave_w(act, 0, 0)
        interleave_w(act, 0, 1)
        interleave_w(act, 0, 2)
        interleave_w(vec, 0, 3)
        gather(2, 2)
        quantise_w(0, 0, 1024)
        for m in range(8):
            multiply(0, m)
        gather(2, 3)
        interleave_x(act, 2, 0)
        interleave_x(vec, 2, 1)
        interleave_w(vec, 1, 0)
        quantise_x(2, 0, 256)
        quantise_x(2, 256, 512)
        for c in range(1, 4):
            interleave_w(act, 1, c)
        for c in range(4):
            quantise_w(1, 256 * c, 256 * (c + 1))
            multiply(1, 2 * c)
            multiply(1, 2 * c + 1)
        interleave_w(vec, 2, 0)
        interleave_w(act, 2, 1)
        quantise_w(2, 0, 256)
        multiply(2, 0)
        multiply(2, 1)
        quantise_w(2, 256, 512)
        multiply(2, 2)
        multiply(2, 3)
        interleave_w(vec, 2, 2)
        interleave_w(act, 2, 3)
        finish(0)
        finish(1)
        quantise_w(2, 512, 768)
        multiply(2, 4)
        multiply(2, 5)
        finish(2)
        finish(3)
        quantise_w(2, 768, 1024)
        multiply(2, 6)
        multiply(2, 7)
        for m in range(4, 8):
            finish(m)
